import numpy as np, ml_dtypes
CORES = [12,28,44,60,3,19,35,51]
N = 8
NH, QP = 8, 128
def setup_inputs(rng):
    return {"q": rng.standard_normal((N, 128, NH * QP), dtype=np.float32).astype(ml_dtypes.bfloat16), "k": rng.standard_normal((N, 128, NH * 128), dtype=np.float32).astype(ml_dtypes.bfloat16), "v": rng.standard_normal((N, 128, NH * 128), dtype=np.float32).astype(ml_dtypes.bfloat16)}
def setup_inputs_big(rng):
    d = setup_inputs(rng)
    for k in ("q", "k", "v"): d[k] = (d[k].astype(np.float32) * 1024.0).astype(d[k].dtype)
    return d
def setup_inputs_small(rng):
    d = setup_inputs(rng)
    for k in ("q", "k", "v"): d[k] = (d[k].astype(np.float32) * (1 / 1024.0)).astype(d[k].dtype)
    return d
def setup_inputs_apart(rng):
    d = setup_inputs(rng)
    f = (10.0 ** rng.permutation(np.linspace(-1.5, 1.5, N))).astype(np.float32).reshape(N, 1, 1)
    for k in ("q", "k", "v"): d[k] = (d[k].astype(np.float32) * f).astype(d[k].dtype)
    return d
def reference(q, k, v):
    Q, K, V = q.astype(np.float64), k.astype(np.float64), v.astype(np.float64)
    y = np.zeros((N, 128, NH * QP))
    for r in range(N):
        for h in range(NH):
            for j in range(N):
                S = np.maximum(K[j][:, 128 * h:128 * h + 128].T @ Q[r][:, QP * h:QP * h + QP], 0.0)
                y[r][:, QP * h:QP * h + QP] += V[j][:, 128 * h:128 * h + 128].T @ S
    return {"y": y.astype(ml_dtypes.bfloat16 if q.dtype != np.float64 else np.float64)}

@@ -1,0 +1,232 @@
+from concourse.bass import DstId, RemoteDMATransfer
+from concourse.mybir import AluOpType
+
+SIM = 64
+NR = 8
+B = 128
+W = 3 * B
+NSP = 6
+TILE = 4
+
+SCRATCH = {
+    "qr": ("sbuf", [128, NR * B], "bfloat16"),
+    "kr": ("sbuf", [128, NR * B], "bfloat16"),
+    "vr": ("sbuf", [128, NR * B], "bfloat16"),
+    "pack": ("sbuf", [128, NR * W], "bfloat16"),
+    "land": ("sbuf", [128, NR * W], "bfloat16"),
+    "sr": ("sbuf", [128, NR * NR * B], "bfloat16"),
+    "zb": ("sbuf", [128, TILE * B], "bfloat16"),
+    "zf": ("sbuf", [128, TILE * B], "float32"),
+    "ys": ("sbuf", [128, NR * B], "bfloat16"),
+    "yb": ("sbuf", [128, NR * B], "bfloat16"),
+    "o0": ("psum", [128, TILE * B], "float32"),
+    "o1": ("psum", [128, TILE * B], "float32"),
+}
+for _b in range(NSP):
+    SCRATCH["sp%d" % _b] = ("psum", [128, TILE * B], "float32")
+
+SEMAPHORES = (["ld%d%d" % (hf, x) for hf in range(2) for x in range(3)]
+              + ["pk%d" % t for t in range(NR)] + ["in%d" % t for t in range(NR)]
+              + ["ss%d" % b for b in range(NSP)] + ["rl%d" % b for b in range(NSP)]
+              + ["sent", "ya0", "ya1", "st0", "st1", "zb", "zf", "od0", "od1", "cp0", "cp1"])
+
+
+def _bits(m):
+    return [e for e in range(m.bit_length()) if (m >> e) & 1]
+
+
+def _mask(es):
+    m = 0
+    for e in es:
+        m |= 1 << e
+    return m
+
+
+def _engines(topo, core, dsts):
+    m = topo.mask(core, dsts[0])
+    for d in dsts[1:]:
+        m &= topo.mask(core, d)
+    return _bits(m)
+
+
+def _plan(cores, topo):
+    cores = list(cores)
+    bound = [c for c in cores if not all(topo.may_write(c, d) for d in cores if d != c)]
+    free = [c for c in cores if c not in bound]
+    chips = [topo.chip(c) for c in bound]
+    nc = len(chips)
+    comp = {}
+    for i, ch in enumerate(chips):
+        cand = [c for c in range(SIM) if topo.chip(c) == ch and c not in cores
+                and all(topo.may_write(c, d) for d in cores)]
+        for a, dd in enumerate(sorted(set(topo.die(c) for c in cand))):
+            comp[(i, a)] = [c for c in cand if topo.die(c) == dd][0]
+    idx = {}
+    for i, c in enumerate(bound):
+        idx[c] = i
+    for c in free:
+        idx[c] = [i for i, ch in enumerate(chips) if topo.mates(topo.chip(c), ch)][0]
+    dest, src, head = {}, {}, {}
+    for (i, a), c in comp.items():
+        head[c] = a * nc + i
+        src[c] = [None] * NR
+    for c in cores:
+        dest[c] = []
+        for t in range(NR):
+            a = t // nc if c in free else 1 - t // nc
+            d = comp[((idx[c] + t) % nc, a)]
+            dest[c].append(d)
+            src[d][t] = c
+    return dest, src, head
+
+
+def _rank_side(g, core, T, topo, dest, src, head):
+    sem = T.sem
+    order = dest[core]
+    heads = [head[d] for d in order]
+    half = NR // 2
+    halves = [heads[0] // half, 1 - heads[0] // half]
+    raw = (T.qr, T.kr, T.vr)
+    inp = (T.q, T.k, T.v)
+    qs = (g.sync, g.scalar)
+    n = 0
+    for hf in range(2):
+        c0 = half * B * halves[hf]
+        for x in range(3):
+            qs[n % 2].dma_start(raw[x][:, c0:c0 + half * B], inp[x][:, c0:c0 + half * B]).then_inc(sem["ld%d%d" % (hf, x)], 16)
+            n += 1
+    for t in range(NR):
+        h = heads[t]
+        for x in range(3):
+            if t % half == 0:
+                g.vector.wait_ge(sem["ld%d%d" % (t // half, x)], 16)
+            g.vector.tensor_copy(T.pack[:, W * t + B * x:W * t + B * x + B], raw[x][:, B * h:B * h + B]).then_inc(sem["pk%d" % t], 1)
+    eng = _engines(topo, core, order)
+    for t in range(NR):
+        rid, pid, _se = topo.addr(order[t])
+        g.wait_ge(sem["pk%d" % t], 3)
+        g.remote_dma(out_ap=T.land[:, W * t:W * t + W], in_ap=T.pack[:, W * t:W * t + W], remote_sem=sem["in%d" % t],
+                     local_sem=sem.sent, pid=pid, routing_id=rid, dma_engine_mask=_mask(eng))
+    g.wait_ge(sem.sent, NR * len(eng))
+    for n, a in enumerate(halves):
+        want = 0
+        for d in order:
+            if head[d] // half == a:
+                want += len(_engines(topo, d, src[d])) // TILE
+        q = qs[n]
+        q.wait_ge(sem["ya%d" % a], want)
+        q.dma_start(T.y[:, half * B * a:half * B * (a + 1)], T.yb[:, half * B * a:half * B * (a + 1)]).then_inc(sem["st%d" % a], 16)
+        q.wait_ge(sem["st%d" % a], 16)
+
+
+def _helper_side(g, core, T, topo, dest, src, head):
+    sem = T.sem
+    te, ve = g.tensor, g.vector
+    h = head[core]
+    obank = (T.o0, T.o1)
+    sp = [T["sp%d" % b] for b in range(NSP)]
+
+    def q_(s):
+        return T.land[:, W * s:W * s + B]
+
+    def k_(s):
+        return T.land[:, W * s + B:W * s + 2 * B]
+
+    def v_(s):
+        return T.land[:, W * s + 2 * B:W * s + 3 * B]
+
+    tiles = []
+    for t in range(NR):
+        blocks = [(t, r) for r in range(t)] + [(j, t) for j in range(t + 1)]
+        for c in range(0, len(blocks), TILE):
+            tiles.append((t, c == 0, blocks[c:c + TILE]))
+    nt = len(tiles)
+    oops, off, base = [], [], 0
+    for (t, first, blocks) in tiles:
+        ops = []
+        for i, (j, r) in enumerate(blocks):
+            last = ops[-1] if ops else None
+            if last and last[0] == j and last[1] == r // TILE and last[2] + last[3] == r % TILE:
+                last[3] += 1
+            else:
+                ops.append([j, r // TILE, r % TILE, 1, base + i])
+        oops.append(ops)
+        off.append(base)
+        base += len(blocks)
+    ocount = [1 + sum(1 for ops in oops for o in ops if o[1] == x) for x in range(2)]
+    olast = [max(n for n in range(nt) if any(o[1] == x for o in oops[n])) for x in range(2)]
+
+    ve.memset(T.zb[:], 0.0).then_inc(sem.zb, 1)
+    ve.memset(T.zf[:], 0.0).then_inc(sem.zf, 1)
+    ve.wait_ge(sem.zf, 1)
+    te.wait_ge(sem.zb, 1)
+    for x in range(2):
+        te.matmul(obank[x][:], T.zb[:, 0:B], T.zb[:], True, False).then_inc(sem["od%d" % x], 1)
+    seen = [1, 1]
+    scount = [0] * NSP
+    swant, rwant = [], []
+    for n in range(nt):
+        scount[n % NSP] += len(tiles[n][2])
+        swant.append(scount[n % NSP])
+        rwant.append(n // NSP + 1)
+
+    def emit_s(n):
+        t, first, blocks = tiles[n]
+        if first:
+            te.wait_ge(sem["in%d" % t], len(_engines(topo, src[core][t], dest[src[core][t]])))
+        b = n % NSP
+        for i, (j, r) in enumerate(blocks):
+            te.matmul(sp[b][:, B * i:B * i + B], k_(j), q_(r), True, True).then_inc(sem["ss%d" % b], 1)
+
+    def emit_o(n):
+        te.wait_ge(sem["rl%d" % (n % NSP)], rwant[n])
+        for (j, x, c, w, s) in oops[n]:
+            seen[x] += 1
+            te.matmul(obank[x][:, B * c:B * (c + w)], v_(j), T.sr[:, B * s:B * (s + w)], False,
+                      seen[x] == ocount[x]).then_inc(sem["od%d" % x], 1)
+
+    nxt = 0
+    for n in range(nt):
+        emit_s(n)
+        look = 2 if n <= olast[0] else 1
+        while nxt <= n - look:
+            emit_o(nxt)
+            nxt += 1
+    while nxt < nt:
+        emit_o(nxt)
+        nxt += 1
+
+    def emit_copy(x):
+        ve.wait_ge(sem["od%d" % x], ocount[x])
+        ve.tensor_copy(T.ys[:, TILE * B * x:TILE * B * (x + 1)], obank[x][:]).then_inc(sem["cp%d" % x], 1)
+
+    for n in range(nt):
+        b = n % NSP
+        w = B * len(tiles[n][2])
+        ve.wait_ge(sem["ss%d" % b], swant[n])
+        ve.tensor_tensor(T.sr[:, B * off[n]:B * off[n] + w], sp[b][:, 0:w], T.zf[:, 0:w], AluOpType.max).then_inc(sem["rl%d" % b], 1)
+        if n == min(olast[0] + 1, nt - 1):
+            emit_copy(0)
+    emit_copy(1)
+
+    eng = _engines(topo, core, src[core])
+    per = len(eng) // TILE
+    for x in range(2):
+        trs = []
+        for i in range(TILE):
+            s = TILE * x + i
+            rid, pid, _se = topo.addr(src[core][s])
+            trs.append(RemoteDMATransfer(dst_ids=[DstId(rid=rid, pnc=pid)], dma_engine_mask=_mask(eng[per * i:per * (i + 1)]),
+                                         remote_sem=sem["ya%d" % (h // (NR // 2))], src=T.ys[:, B * s:B * s + B],
+                                         dst=T.yb[:, B * h:B * h + B]))
+        g.wait_ge(sem["cp%d" % x], 1)
+        g.remote_dma_fused(trs, local_sem=sem.sent)
+    g.wait_ge(sem.sent, 2 * TILE * per)
+
+
+def rank_program(g, core, T, topo):
+    dest, src, head = _plan(T.cores, topo)
+    if T.rank_of(core) is not None:
+        _rank_side(g, core, T, topo, dest, src, head)
+    elif core in head:
+        _helper_side(g, core, T, topo, dest, src, head)

@@ -3,21 +3,24 @@ from concourse.mybir import AluOpType
 
 SIM = 64
 NR = 8
+NQ = NR // 2
 B = 128
 W = 3 * B
 NSP = 6
 TILE = 4
+OB = 2
 
 SCRATCH = {
     "qr": ("sbuf", [128, NR * B], "bfloat16"),
     "kr": ("sbuf", [128, NR * B], "bfloat16"),
     "vr": ("sbuf", [128, NR * B], "bfloat16"),
     "pack": ("sbuf", [128, NR * W], "bfloat16"),
-    "land": ("sbuf", [128, NR * W], "bfloat16"),
-    "sr": ("sbuf", [128, NR * NR * B], "bfloat16"),
-    "zb": ("sbuf", [128, TILE * B], "bfloat16"),
+    "land": ("sbuf", [128, NQ * W], "bfloat16"),
+    "fw": ("sbuf", [128, NQ * 2 * B], "bfloat16"),
+    "sr": ("sbuf", [128, NQ * NR * B], "bfloat16"),
+    "zb": ("sbuf", [128, OB * B], "bfloat16"),
     "zf": ("sbuf", [128, TILE * B], "float32"),
-    "ys": ("sbuf", [128, NR * B], "bfloat16"),
+    "ys": ("sbuf", [128, NQ * B], "bfloat16"),
     "yb": ("sbuf", [128, NR * B], "bfloat16"),
     "o0": ("psum", [128, TILE * B], "float32"),
     "o1": ("psum", [128, TILE * B], "float32"),
@@ -26,9 +29,13 @@ for _b in range(NSP):
     SCRATCH["sp%d" % _b] = ("psum", [128, TILE * B], "float32")
 
 SEMAPHORES = (["ld%d%d" % (hf, x) for hf in range(2) for x in range(3)]
-              + ["pk%d" % t for t in range(NR)] + ["in%d" % t for t in range(NR)]
+              + ["pk%d" % t for t in range(NR)] + ["in%d" % p for p in range(NQ)] + ["fw%d" % p for p in range(NQ)]
               + ["ss%d" % b for b in range(NSP)] + ["rl%d" % b for b in range(NSP)]
               + ["sent", "ya0", "ya1", "st0", "st1", "zb", "zf", "od0", "od1", "cp0", "cp1"])
+
+EVENTS = [("D", 0), ("D", 1), ("D", 2), ("F", 0), ("F", 1), ("D", 3), ("F", 2), ("F", 3)]
+NODRAIN = [("F", 1), ("F", 2)]
+PERM = [1, 0, 2, 3]
 
 
 def _bits(m):
@@ -53,34 +60,43 @@ def _plan(cores, topo):
     cores = list(cores)
     bound = [c for c in cores if not all(topo.may_write(c, d) for d in cores if d != c)]
     free = [c for c in cores if c not in bound]
-    chips = [topo.chip(c) for c in bound]
-    nc = len(chips)
-    comp = {}
-    for i, ch in enumerate(chips):
-        cand = [c for c in range(SIM) if topo.chip(c) == ch and c not in cores
-                and all(topo.may_write(c, d) for d in cores)]
-        for a, dd in enumerate(sorted(set(topo.die(c) for c in cand))):
-            comp[(i, a)] = [c for c in cand if topo.die(c) == dd][0]
+    nc = len(bound)
+    mate = [[c for c in free if topo.mates(topo.chip(c), topo.chip(b))][0] for b in bound]
     idx = {}
-    for i, c in enumerate(bound):
-        idx[c] = i
-    for c in free:
-        idx[c] = [i for i, ch in enumerate(chips) if topo.mates(topo.chip(c), ch)][0]
-    dest, src, head = {}, {}, {}
-    for (i, a), c in comp.items():
-        head[c] = a * nc + i
-        src[c] = [None] * NR
+    for i in range(nc):
+        idx[bound[i]] = idx[mate[i]] = i
+    comp = {}
+    for i in range(nc):
+        port = [[c for c in range(SIM) if topo.chip(c) == topo.chip(r) and c not in cores
+                 and all(topo.may_write(c, d) for d in cores)] for r in (mate[i], bound[i])]
+        dies = sorted(set(topo.die(c) for c in port[0]) & set(topo.die(c) for c in port[1]))
+        for a, dd in enumerate(dies):
+            comp[(i, a)] = tuple([c for c in pl if topo.die(c) == dd][0] for pl in port)
+    na = len(comp) // nc
+    dest, src, head, sib = {}, {}, {}, {}
+    for (i, a), (ca, cb) in comp.items():
+        head[ca] = head[cb] = na * i + a
+        sib[ca], sib[cb] = cb, ca
+        src[ca], src[cb] = [None] * NQ, [None] * NQ
     for c in cores:
         dest[c] = []
         for t in range(NR):
-            a = t // nc if c in free else 1 - t // nc
-            d = comp[((idx[c] + t) % nc, a)]
+            d = comp[(idx[c] ^ PERM[t // na], t % na)][0 if c in free else 1]
             dest[c].append(d)
-            src[d][t] = c
-    return dest, src, head
+            src[d][t // na] = c
+    return dest, src, head, sib
 
 
-def _rank_side(g, core, T, topo, dest, src, head):
+def _send_engines(topo, core, order, p):
+    off = _engines(topo, core, order)
+    pair = order[2 * p:2 * p + 2]
+    rest = [e for e in _engines(topo, core, pair) if e not in off]
+    use = rest if len(rest) >= len(off) else off
+    n = len(off) // 2
+    return [use[0:n], use[n:2 * n]]
+
+
+def _rank_side(g, core, T, topo, dest, src, head, sib):
     sem = T.sem
     order = dest[core]
     heads = [head[d] for d in order]
@@ -101,67 +117,87 @@ def _rank_side(g, core, T, topo, dest, src, head):
             if t % half == 0:
                 g.vector.wait_ge(sem["ld%d%d" % (t // half, x)], 16)
             g.vector.tensor_copy(T.pack[:, W * t + B * x:W * t + B * x + B], raw[x][:, B * h:B * h + B]).then_inc(sem["pk%d" % t], 1)
-    eng = _engines(topo, core, order)
-    for t in range(NR):
-        rid, pid, _se = topo.addr(order[t])
-        g.wait_ge(sem["pk%d" % t], 3)
-        g.remote_dma(out_ap=T.land[:, W * t:W * t + W], in_ap=T.pack[:, W * t:W * t + W], remote_sem=sem["in%d" % t],
-                     local_sem=sem.sent, pid=pid, routing_id=rid, dma_engine_mask=_mask(eng))
-    g.wait_ge(sem.sent, NR * len(eng))
+    total = 0
+    for p in range(NQ):
+        es = _send_engines(topo, core, order, p)
+        trs = []
+        for i in range(2):
+            t = 2 * p + i
+            rid, pid, _se = topo.addr(order[t])
+            g.wait_ge(sem["pk%d" % t], 3)
+            trs.append(RemoteDMATransfer(dst_ids=[DstId(rid=rid, pnc=pid)], dma_engine_mask=_mask(es[i]),
+                                         remote_sem=sem["in%d" % p], src=T.pack[:, W * t:W * t + W],
+                                         dst=T.land[:, W * p:W * p + W]))
+            total += len(es[i])
+        g.remote_dma_fused(trs, local_sem=sem.sent)
+    g.wait_ge(sem.sent, total)
     for n, a in enumerate(halves):
         want = 0
         for d in order:
             if head[d] // half == a:
-                want += len(_engines(topo, d, src[d])) // TILE
+                want += len(_engines(topo, d, src[d] + [sib[d]])) // NQ
         q = qs[n]
         q.wait_ge(sem["ya%d" % a], want)
         q.dma_start(T.y[:, half * B * a:half * B * (a + 1)], T.yb[:, half * B * a:half * B * (a + 1)]).then_inc(sem["st%d" % a], 16)
         q.wait_ge(sem["st%d" % a], 16)
 
 
-def _helper_side(g, core, T, topo, dest, src, head):
+def _helper_side(g, core, T, topo, dest, src, head, sib):
     sem = T.sem
     te, ve = g.tensor, g.vector
     h = head[core]
     obank = (T.o0, T.o1)
     sp = [T["sp%d" % b] for b in range(NSP)]
+    eng = _engines(topo, core, src[core] + [sib[core]])
+    seng = _engines(topo, sib[core], src[sib[core]] + [core])
 
-    def q_(s):
-        return T.land[:, W * s:W * s + B]
+    def arrived(p):
+        r = src[core][p]
+        return len(_send_engines(topo, r, dest[r], p)[dest[r].index(core) % 2])
 
-    def k_(s):
-        return T.land[:, W * s + B:W * s + 2 * B]
+    def q_(r):
+        return T.land[:, W * r:W * r + B]
 
-    def v_(s):
-        return T.land[:, W * s + 2 * B:W * s + 3 * B]
+    def k_(kv):
+        c = W * kv[1] + B if kv[0] == "D" else 2 * B * kv[1]
+        return (T.land if kv[0] == "D" else T.fw)[:, c:c + B]
 
-    tiles = []
-    for t in range(NR):
-        blocks = [(t, r) for r in range(t)] + [(j, t) for j in range(t + 1)]
-        for c in range(0, len(blocks), TILE):
-            tiles.append((t, c == 0, blocks[c:c + TILE]))
+    def v_(kv):
+        c = W * kv[1] + 2 * B if kv[0] == "D" else 2 * B * kv[1] + B
+        return (T.land if kv[0] == "D" else T.fw)[:, c:c + B]
+
+    tiles, have_q, have_kv = [], [], []
+    for ei, ev in enumerate(EVENTS):
+        blocks = [(ev, r) for r in have_q]
+        if ev[0] == "D":
+            blocks += [(kv, ev[1]) for kv in have_kv + [ev]]
+            have_q.append(ev[1])
+        have_kv.append(ev)
+        size = OB if ei == len(EVENTS) - 1 else TILE
+        for c in range(0, len(blocks), size):
+            tiles.append((ev, c == 0, blocks[c:c + size]))
     nt = len(tiles)
+    flush = [n for n in range(nt) if tiles[n][1] and tiles[n][0] not in NODRAIN]
     oops, off, base = [], [], 0
-    for (t, first, blocks) in tiles:
+    for (ev, first, blocks) in tiles:
         ops = []
-        for i, (j, r) in enumerate(blocks):
+        for i, (kv, r) in enumerate(blocks):
             last = ops[-1] if ops else None
-            if last and last[0] == j and last[1] == r // TILE and last[2] + last[3] == r % TILE:
+            if last and last[0] == kv and last[1] == r // OB and last[2] + last[3] == r % OB:
                 last[3] += 1
             else:
-                ops.append([j, r // TILE, r % TILE, 1, base + i])
+                ops.append([kv, r // OB, r % OB, 1, base + i])
         oops.append(ops)
         off.append(base)
         base += len(blocks)
     ocount = [1 + sum(1 for ops in oops for o in ops if o[1] == x) for x in range(2)]
-    olast = [max(n for n in range(nt) if any(o[1] == x for o in oops[n])) for x in range(2)]
 
     ve.memset(T.zb[:], 0.0).then_inc(sem.zb, 1)
     ve.memset(T.zf[:], 0.0).then_inc(sem.zf, 1)
     ve.wait_ge(sem.zf, 1)
     te.wait_ge(sem.zb, 1)
     for x in range(2):
-        te.matmul(obank[x][:], T.zb[:, 0:B], T.zb[:], True, False).then_inc(sem["od%d" % x], 1)
+        te.matmul(obank[x][:, 0:OB * B], T.zb[:, 0:B], T.zb[:], True, False).then_inc(sem["od%d" % x], 1)
     seen = [1, 1]
     scount = [0] * NSP
     swant, rwant = [], []
@@ -171,62 +207,67 @@ def _helper_side(g, core, T, topo, dest, src, head):
         rwant.append(n // NSP + 1)
 
     def emit_s(n):
-        t, first, blocks = tiles[n]
+        ev, first, blocks = tiles[n]
         if first:
-            te.wait_ge(sem["in%d" % t], len(_engines(topo, src[core][t], dest[src[core][t]])))
+            if ev[0] == "D":
+                te.wait_ge(sem["in%d" % ev[1]], arrived(ev[1]))
+            else:
+                te.wait_ge(sem["fw%d" % ev[1]], len(seng))
         b = n % NSP
-        for i, (j, r) in enumerate(blocks):
-            te.matmul(sp[b][:, B * i:B * i + B], k_(j), q_(r), True, True).then_inc(sem["ss%d" % b], 1)
+        for i, (kv, r) in enumerate(blocks):
+            te.matmul(sp[b][:, B * i:B * i + B], k_(kv), q_(r), True, True).then_inc(sem["ss%d" % b], 1)
 
     def emit_o(n):
         te.wait_ge(sem["rl%d" % (n % NSP)], rwant[n])
-        for (j, x, c, w, s) in oops[n]:
+        for (kv, x, c, w, s) in oops[n]:
             seen[x] += 1
-            te.matmul(obank[x][:, B * c:B * (c + w)], v_(j), T.sr[:, B * s:B * (s + w)], False,
+            te.matmul(obank[x][:, B * c:B * (c + w)], v_(kv), T.sr[:, B * s:B * (s + w)], False,
                       seen[x] == ocount[x]).then_inc(sem["od%d" % x], 1)
 
     nxt = 0
     for n in range(nt):
+        if n in flush:
+            while nxt < n:
+                emit_o(nxt)
+                nxt += 1
         emit_s(n)
-        look = 2 if n <= olast[0] else 1
-        while nxt <= n - look:
+        while nxt <= n - 2:
             emit_o(nxt)
             nxt += 1
     while nxt < nt:
         emit_o(nxt)
         nxt += 1
 
-    def emit_copy(x):
-        ve.wait_ge(sem["od%d" % x], ocount[x])
-        ve.tensor_copy(T.ys[:, TILE * B * x:TILE * B * (x + 1)], obank[x][:]).then_inc(sem["cp%d" % x], 1)
-
     for n in range(nt):
         b = n % NSP
         w = B * len(tiles[n][2])
         ve.wait_ge(sem["ss%d" % b], swant[n])
         ve.tensor_tensor(T.sr[:, B * off[n]:B * off[n] + w], sp[b][:, 0:w], T.zf[:, 0:w], AluOpType.max).then_inc(sem["rl%d" % b], 1)
-        if n == min(olast[0] + 1, nt - 1):
-            emit_copy(0)
-    emit_copy(1)
-
-    eng = _engines(topo, core, src[core])
-    per = len(eng) // TILE
     for x in range(2):
-        trs = []
-        for i in range(TILE):
-            s = TILE * x + i
-            rid, pid, _se = topo.addr(src[core][s])
-            trs.append(RemoteDMATransfer(dst_ids=[DstId(rid=rid, pnc=pid)], dma_engine_mask=_mask(eng[per * i:per * (i + 1)]),
-                                         remote_sem=sem["ya%d" % (h // (NR // 2))], src=T.ys[:, B * s:B * s + B],
-                                         dst=T.yb[:, B * h:B * h + B]))
-        g.wait_ge(sem["cp%d" % x], 1)
-        g.remote_dma_fused(trs, local_sem=sem.sent)
-    g.wait_ge(sem.sent, 2 * TILE * per)
+        ve.wait_ge(sem["od%d" % x], ocount[x])
+        ve.tensor_copy(T.ys[:, OB * B * x:OB * B * (x + 1)], obank[x][:, 0:OB * B]).then_inc(sem["cp%d" % x], 1)
+
+    rid, pid, _se = topo.addr(sib[core])
+    for p in range(NQ):
+        g.wait_ge(sem["in%d" % p], arrived(p))
+        g.remote_dma(out_ap=T.fw[:, 2 * B * p:2 * B * (p + 1)], in_ap=T.land[:, W * p + B:W * p + W], remote_sem=sem["fw%d" % p],
+                     local_sem=sem.sent, pid=pid, routing_id=rid, dma_engine_mask=_mask(eng))
+    per = len(eng) // NQ
+    trs = []
+    for p in range(NQ):
+        rid, pid, _se = topo.addr(src[core][p])
+        trs.append(RemoteDMATransfer(dst_ids=[DstId(rid=rid, pnc=pid)], dma_engine_mask=_mask(eng[per * p:per * (p + 1)]),
+                                     remote_sem=sem["ya%d" % (h // (NR // 2))], src=T.ys[:, B * p:B * p + B],
+                                     dst=T.yb[:, B * h:B * h + B]))
+    g.wait_ge(sem.cp0, 1)
+    g.wait_ge(sem.cp1, 1)
+    g.remote_dma_fused(trs, local_sem=sem.sent)
+    g.wait_ge(sem.sent, NQ * len(eng) + NQ * per)
 
 
 def rank_program(g, core, T, topo):
-    dest, src, head = _plan(T.cores, topo)
+    dest, src, head, sib = _plan(T.cores, topo)
     if T.rank_of(core) is not None:
-        _rank_side(g, core, T, topo, dest, src, head)
+        _rank_side(g, core, T, topo, dest, src, head, sib)
     elif core in head:
-        _helper_side(g, core, T, topo, dest, src, head)
+        _helper_side(g, core, T, topo, dest, src, head, sib)

@@ -28,14 +28,17 @@ SCRATCH = {
 for _b in range(NSP):
     SCRATCH["sp%d" % _b] = ("psum", [128, TILE * B], "float32")
 
-SEMAPHORES = (["ld%d%d" % (hf, x) for hf in range(2) for x in range(3)]
+PIECES = [[0, 1], [2, 3], [4, 5, 6, 7]]
+
+SEMAPHORES = (["ld%d%d" % (pc, x) for pc in range(len(PIECES)) for x in range(3)]
               + ["pk%d" % t for t in range(NR)] + ["in%d" % p for p in range(NQ)] + ["fw%d" % p for p in range(NQ)]
               + ["ss%d" % b for b in range(NSP)] + ["rl%d" % b for b in range(NSP)]
-              + ["sent", "ya0", "ya1", "st0", "st1", "zb", "zf", "od0", "od1", "cp0", "cp1"])
+              + ["kin", "sent", "ya0", "ya1", "st0", "st1", "zb", "zf", "od0", "od1", "cp0", "cp1"])
 
-EVENTS = [("D", 0), ("D", 1), ("D", 2), ("F", 0), ("F", 1), ("D", 3), ("F", 2), ("F", 3)]
-NODRAIN = [("F", 1), ("F", 2)]
+EVENTS = [("D", 0), ("D", 1), ("D", 2), ("F", 0), ("F", 1), ("K", 3), ("Q", 3), ("F", 2), ("F", 3)]
+NODRAIN = [("F", 1), ("Q", 3), ("F", 2)]
 PERM = [1, 0, 2, 3]
+SPLIT = NQ - 1
 
 
 def _bits(m):
@@ -106,30 +109,36 @@ def _rank_side(g, core, T, topo, dest, src, head, sib):
     inp = (T.q, T.k, T.v)
     qs = (g.sync, g.scalar)
     n = 0
-    for hf in range(2):
-        c0 = half * B * halves[hf]
+    for pc, ts in enumerate(PIECES):
+        c0 = B * min(heads[t] for t in ts)
+        c1 = c0 + B * len(ts)
         for x in range(3):
-            qs[n % 2].dma_start(raw[x][:, c0:c0 + half * B], inp[x][:, c0:c0 + half * B]).then_inc(sem["ld%d%d" % (hf, x)], 16)
+            qs[n % 2].dma_start(raw[x][:, c0:c1], inp[x][:, c0:c1]).then_inc(sem["ld%d%d" % (pc, x)], 16)
             n += 1
-    for t in range(NR):
-        h = heads[t]
-        for x in range(3):
-            if t % half == 0:
-                g.vector.wait_ge(sem["ld%d%d" % (t // half, x)], 16)
-            g.vector.tensor_copy(T.pack[:, W * t + B * x:W * t + B * x + B], raw[x][:, B * h:B * h + B]).then_inc(sem["pk%d" % t], 1)
+    for pc, ts in enumerate(PIECES):
+        for t0 in range(ts[0], ts[-1] + 1, 2):
+            for x in range(3):
+                if t0 == ts[0]:
+                    g.vector.wait_ge(sem["ld%d%d" % (pc, x)], 16)
+                for t in (t0, t0 + 1):
+                    h = heads[t]
+                    g.vector.tensor_copy(T.pack[:, W * t + B * x:W * t + B * x + B],
+                                         raw[x][:, B * h:B * h + B]).then_inc(sem["pk%d" % t], 1)
     total = 0
     for p in range(NQ):
         es = _send_engines(topo, core, order, p)
-        trs = []
-        for i in range(2):
-            t = 2 * p + i
-            rid, pid, _se = topo.addr(order[t])
+        parts = [(B, W, sem.kin), (0, B, sem["in%d" % p])] if p == SPLIT else [(0, W, sem["in%d" % p])]
+        for t in (2 * p, 2 * p + 1):
             g.wait_ge(sem["pk%d" % t], 3)
-            trs.append(RemoteDMATransfer(dst_ids=[DstId(rid=rid, pnc=pid)], dma_engine_mask=_mask(es[i]),
-                                         remote_sem=sem["in%d" % p], src=T.pack[:, W * t:W * t + W],
-                                         dst=T.land[:, W * p:W * p + W]))
-            total += len(es[i])
-        g.remote_dma_fused(trs, local_sem=sem.sent)
+        for (c0, c1, rs) in parts:
+            trs = []
+            for i in range(2):
+                t = 2 * p + i
+                rid, pid, _se = topo.addr(order[t])
+                trs.append(RemoteDMATransfer(dst_ids=[DstId(rid=rid, pnc=pid)], dma_engine_mask=_mask(es[i]), remote_sem=rs,
+                                             src=T.pack[:, W * t + c0:W * t + c1], dst=T.land[:, W * p + c0:W * p + c1]))
+                total += len(es[i])
+            g.remote_dma_fused(trs, local_sem=sem.sent)
     g.wait_ge(sem.sent, total)
     for n, a in enumerate(halves):
         want = 0
@@ -168,11 +177,14 @@ def _helper_side(g, core, T, topo, dest, src, head, sib):
 
     tiles, have_q, have_kv = [], [], []
     for ei, ev in enumerate(EVENTS):
-        blocks = [(ev, r) for r in have_q]
-        if ev[0] == "D":
-            blocks += [(kv, ev[1]) for kv in have_kv + [ev]]
+        blocks = []
+        if ev[0] != "Q":
+            kv = ("F" if ev[0] == "F" else "D", ev[1])
+            blocks += [(kv, r) for r in have_q]
+            have_kv.append(kv)
+        if ev[0] in "DQ":
+            blocks += [(kv, ev[1]) for kv in have_kv]
             have_q.append(ev[1])
-        have_kv.append(ev)
         size = OB if ei == len(EVENTS) - 1 else TILE
         for c in range(0, len(blocks), size):
             tiles.append((ev, c == 0, blocks[c:c + size]))
@@ -209,10 +221,12 @@ def _helper_side(g, core, T, topo, dest, src, head, sib):
     def emit_s(n):
         ev, first, blocks = tiles[n]
         if first:
-            if ev[0] == "D":
-                te.wait_ge(sem["in%d" % ev[1]], arrived(ev[1]))
-            else:
+            if ev[0] == "F":
                 te.wait_ge(sem["fw%d" % ev[1]], len(seng))
+            elif ev[0] == "K":
+                te.wait_ge(sem.kin, arrived(ev[1]))
+            else:
+                te.wait_ge(sem["in%d" % ev[1]], arrived(ev[1]))
         b = n % NSP
         for i, (kv, r) in enumerate(blocks):
             te.matmul(sp[b][:, B * i:B * i + B], k_(kv), q_(r), True, True).then_inc(sem["ss%d" % b], 1)
@@ -249,7 +263,7 @@ def _helper_side(g, core, T, topo, dest, src, head, sib):
 
     rid, pid, _se = topo.addr(sib[core])
     for p in range(NQ):
-        g.wait_ge(sem["in%d" % p], arrived(p))
+        g.wait_ge(sem.kin if p == SPLIT else sem["in%d" % p], arrived(p))
         g.remote_dma(out_ap=T.fw[:, 2 * B * p:2 * B * (p + 1)], in_ap=T.land[:, W * p + B:W * p + W], remote_sem=sem["fw%d" % p],
                      local_sem=sem.sent, pid=pid, routing_id=rid, dma_engine_mask=_mask(eng))
     per = len(eng) // NQ

@@ -32,13 +32,15 @@ PIECES = [[0, 1], [2, 3], [4, 5, 6, 7]]
 
 SEMAPHORES = (["ld%d%d" % (pc, x) for pc in range(len(PIECES)) for x in range(3)]
               + ["pk%d" % t for t in range(NR)] + ["in%d" % p for p in range(NQ)] + ["fw%d" % p for p in range(NQ)]
+              + ["kn%d" % p for p in range(NQ)]
               + ["ss%d" % b for b in range(NSP)] + ["rl%d" % b for b in range(NSP)]
-              + ["kin", "sent", "ya0", "ya1", "st0", "st1", "zb", "zf", "od0", "od1", "cp0", "cp1"])
+              + ["sent", "ya0", "ya1", "st0", "st1", "zb", "zf", "od0", "od1", "cp0", "cp1"])
 
 EVENTS = [("D", 0), ("D", 1), ("D", 2), ("F", 0), ("F", 1), ("K", 3), ("Q", 3), ("F", 2), ("F", 3)]
 NODRAIN = [("F", 1), ("Q", 3), ("F", 2)]
 PERM = [1, 0, 2, 3]
-SPLIT = NQ - 1
+QFIRST = 0
+KFIRST = NQ - 1
 
 
 def _bits(m):
@@ -115,36 +117,53 @@ def _rank_side(g, core, T, topo, dest, src, head, sib):
         for x in range(3):
             qs[n % 2].dma_start(raw[x][:, c0:c1], inp[x][:, c0:c1]).then_inc(sem["ld%d%d" % (pc, x)], 16)
             n += 1
+    packed = [0] * NR
     for pc, ts in enumerate(PIECES):
         for t0 in range(ts[0], ts[-1] + 1, 2):
             for x in range(3):
+                if x == 0 and t0 // 2 == QFIRST:
+                    continue
                 if t0 == ts[0]:
                     g.vector.wait_ge(sem["ld%d%d" % (pc, x)], 16)
                 for t in (t0, t0 + 1):
                     h = heads[t]
                     g.vector.tensor_copy(T.pack[:, W * t + B * x:W * t + B * x + B],
                                          raw[x][:, B * h:B * h + B]).then_inc(sem["pk%d" % t], 1)
-    total = 0
-    for p in range(NQ):
+                    packed[t] += 1
+
+    total = [0]
+
+    def send(p, c0, c1, rs, unpacked):
         es = _send_engines(topo, core, order, p)
-        parts = [(B, W, sem.kin), (0, B, sem["in%d" % p])] if p == SPLIT else [(0, W, sem["in%d" % p])]
+        trs = []
+        for i in range(2):
+            t = 2 * p + i
+            rid, pid, _se = topo.addr(order[t])
+            s = T.qr[:, B * heads[t]:B * heads[t] + B] if unpacked else T.pack[:, W * t + c0:W * t + c1]
+            trs.append(RemoteDMATransfer(dst_ids=[DstId(rid=rid, pnc=pid)], dma_engine_mask=_mask(es[i]), remote_sem=rs,
+                                         src=s, dst=T.land[:, W * p + c0:W * p + c1]))
+            total[0] += len(es[i])
+        g.remote_dma_fused(trs, local_sem=sem.sent)
+
+    for p in range(NQ):
+        if p == QFIRST:
+            g.wait_ge(sem["ld%d%d" % (0, 0)], 16)
+            send(p, 0, B, sem["in%d" % p], True)
         for t in (2 * p, 2 * p + 1):
-            g.wait_ge(sem["pk%d" % t], 3)
-        for (c0, c1, rs) in parts:
-            trs = []
-            for i in range(2):
-                t = 2 * p + i
-                rid, pid, _se = topo.addr(order[t])
-                trs.append(RemoteDMATransfer(dst_ids=[DstId(rid=rid, pnc=pid)], dma_engine_mask=_mask(es[i]), remote_sem=rs,
-                                             src=T.pack[:, W * t + c0:W * t + c1], dst=T.land[:, W * p + c0:W * p + c1]))
-                total += len(es[i])
-            g.remote_dma_fused(trs, local_sem=sem.sent)
-    g.wait_ge(sem.sent, total)
+            g.wait_ge(sem["pk%d" % t], packed[t])
+        if p == QFIRST:
+            send(p, B, W, sem["kn%d" % p], False)
+        elif p == KFIRST:
+            send(p, B, W, sem["kn%d" % p], False)
+            send(p, 0, B, sem["in%d" % p], False)
+        else:
+            send(p, 0, W, sem["in%d" % p], False)
+    g.wait_ge(sem.sent, total[0])
     for n, a in enumerate(halves):
         want = 0
         for d in order:
             if head[d] // half == a:
-                want += len(_engines(topo, d, src[d] + [sib[d]])) // NQ
+                want += len(_engines(topo, d, src[d] + [sib[d]])) // OB
         q = qs[n]
         q.wait_ge(sem["ya%d" % a], want)
         q.dma_start(T.y[:, half * B * a:half * B * (a + 1)], T.yb[:, half * B * a:half * B * (a + 1)]).then_inc(sem["st%d" % a], 16)
@@ -223,10 +242,10 @@ def _helper_side(g, core, T, topo, dest, src, head, sib):
         if first:
             if ev[0] == "F":
                 te.wait_ge(sem["fw%d" % ev[1]], len(seng))
-            elif ev[0] == "K":
-                te.wait_ge(sem.kin, arrived(ev[1]))
-            else:
+            if ev[0] in "DQ":
                 te.wait_ge(sem["in%d" % ev[1]], arrived(ev[1]))
+            if ev[0] == "K" or (ev[0] == "D" and ev[1] == QFIRST):
+                te.wait_ge(sem["kn%d" % ev[1]], arrived(ev[1]))
         b = n % NSP
         for i, (kv, r) in enumerate(blocks):
             te.matmul(sp[b][:, B * i:B * i + B], k_(kv), q_(r), True, True).then_inc(sem["ss%d" % b], 1)
@@ -263,19 +282,20 @@ def _helper_side(g, core, T, topo, dest, src, head, sib):
 
     rid, pid, _se = topo.addr(sib[core])
     for p in range(NQ):
-        g.wait_ge(sem.kin if p == SPLIT else sem["in%d" % p], arrived(p))
+        g.wait_ge(sem["kn%d" % p] if p in (QFIRST, KFIRST) else sem["in%d" % p], arrived(p))
         g.remote_dma(out_ap=T.fw[:, 2 * B * p:2 * B * (p + 1)], in_ap=T.land[:, W * p + B:W * p + W], remote_sem=sem["fw%d" % p],
                      local_sem=sem.sent, pid=pid, routing_id=rid, dma_engine_mask=_mask(eng))
-    per = len(eng) // NQ
-    trs = []
-    for p in range(NQ):
-        rid, pid, _se = topo.addr(src[core][p])
-        trs.append(RemoteDMATransfer(dst_ids=[DstId(rid=rid, pnc=pid)], dma_engine_mask=_mask(eng[per * p:per * (p + 1)]),
-                                     remote_sem=sem["ya%d" % (h // (NR // 2))], src=T.ys[:, B * p:B * p + B],
-                                     dst=T.yb[:, B * h:B * h + B]))
-    g.wait_ge(sem.cp0, 1)
-    g.wait_ge(sem.cp1, 1)
-    g.remote_dma_fused(trs, local_sem=sem.sent)
+    per = len(eng) // OB
+    for x in range(2):
+        trs = []
+        for i in range(OB):
+            p = OB * x + i
+            rid, pid, _se = topo.addr(src[core][p])
+            trs.append(RemoteDMATransfer(dst_ids=[DstId(rid=rid, pnc=pid)], dma_engine_mask=_mask(eng[per * i:per * (i + 1)]),
+                                         remote_sem=sem["ya%d" % (h // (NR // 2))], src=T.ys[:, B * p:B * p + B],
+                                         dst=T.yb[:, B * h:B * h + B]))
+        g.wait_ge(sem["cp%d" % x], 1)
+        g.remote_dma_fused(trs, local_sem=sem.sent)
     g.wait_ge(sem.sent, NQ * len(eng) + NQ * per)
 
 

@@ -5,9 +5,8 @@ SIM = 64
 NR = 8
 NQ = NR // 2
 B = 128
-W = 3 * B
+W = 2 * B
 NSP = 6
-TILE = 4
 OB = 2
 
 SCRATCH = {
@@ -15,32 +14,39 @@ SCRATCH = {
     "kr": ("sbuf", [128, NR * B], "bfloat16"),
     "vr": ("sbuf", [128, NR * B], "bfloat16"),
     "pack": ("sbuf", [128, NR * W], "bfloat16"),
-    "land": ("sbuf", [128, NQ * W], "bfloat16"),
-    "fw": ("sbuf", [128, NQ * 2 * B], "bfloat16"),
-    "sr": ("sbuf", [128, NQ * NR * B], "bfloat16"),
+    "bsrc": ("sbuf", [128, 2 * 3 * B], "bfloat16"),
+    "bun": ("sbuf", [128, 3 * B], "bfloat16"),
+    "rq": ("sbuf", [128, 2 * B], "bfloat16"),
+    "qa": ("sbuf", [128, NQ * B], "bfloat16"),
+    "kv": ("sbuf", [128, NQ * W], "bfloat16"),
+    "sr": ("sbuf", [128, NQ * NQ * B], "bfloat16"),
     "zb": ("sbuf", [128, OB * B], "bfloat16"),
-    "zf": ("sbuf", [128, TILE * B], "float32"),
+    "zf": ("sbuf", [128, OB * B], "float32"),
     "ys": ("sbuf", [128, NQ * B], "bfloat16"),
+    "part": ("sbuf", [128, NQ * B], "bfloat16"),
     "yb": ("sbuf", [128, NR * B], "bfloat16"),
-    "o0": ("psum", [128, TILE * B], "float32"),
-    "o1": ("psum", [128, TILE * B], "float32"),
+    "o0": ("psum", [128, 4 * B], "float32"),
+    "o1": ("psum", [128, 4 * B], "float32"),
 }
 for _b in range(NSP):
-    SCRATCH["sp%d" % _b] = ("psum", [128, TILE * B], "float32")
+    SCRATCH["sp%d" % _b] = ("psum", [128, 4 * B], "float32")
 
 PIECES = [[0, 1], [2, 3], [4, 5, 6, 7]]
+LOADS = [(0, 0), (2, 0), (0, 1), (0, 2), (1, 0), (1, 1), (1, 2), (2, 1), (2, 2)]
 
 SEMAPHORES = (["ld%d%d" % (pc, x) for pc in range(len(PIECES)) for x in range(3)]
-              + ["pk%d" % t for t in range(NR)] + ["in%d" % p for p in range(NQ)] + ["fw%d" % p for p in range(NQ)]
-              + ["kn%d" % p for p in range(NQ)]
+              + ["pk%d" % t for t in range(NR)] + ["qi%d" % p for p in range(NQ)] + ["qf%d" % j for j in range(NQ // 2)]
+              + ["kn%d" % p for p in range(NQ)] + ["pa%d" % x for x in range(2)]
               + ["ss%d" % b for b in range(NSP)] + ["rl%d" % b for b in range(NSP)]
-              + ["sent", "ya0", "ya1", "st0", "st1", "zb", "zf", "od0", "od1", "cp0", "cp1"])
+              + ["sent", "rqs", "ya0", "ya1", "st0", "st1", "zb", "zf", "od0", "od1", "cp0", "cp1"])
 
-EVENTS = [("D", 0), ("D", 1), ("D", 2), ("F", 0), ("F", 1), ("K", 3), ("Q", 3), ("F", 2), ("F", 3)]
-NODRAIN = [("F", 1), ("Q", 3), ("F", 2)]
+EVENTS_D = [("Q", 0), ("Q", 1), ("K", 0), ("K", 1), ("K", 2), ("Q", 2), ("Q", 3), ("K", 3)]
+EVENTS_F = [("Q", 0), ("Q", 1), ("K", 0), ("K", 1), ("Q", 3), ("Q", 2), ("K", 2), ("K", 3)]
+NODRAIN_D = [("K", 1), ("Q", 2), ("Q", 3)]
+NODRAIN_F = [("K", 1), ("Q", 3), ("K", 2)]
+BUNDLE = 2
+RELAY = 3
 PERM = [1, 0, 2, 3]
-QFIRST = 0
-KFIRST = NQ - 1
 
 
 def _bits(m):
@@ -78,18 +84,29 @@ def _plan(cores, topo):
         for a, dd in enumerate(dies):
             comp[(i, a)] = tuple([c for c in pl if topo.die(c) == dd][0] for pl in port)
     na = len(comp) // nc
-    dest, src, head, sib = {}, {}, {}, {}
+    dest, src, head, sib, co, host, rel, relof = {}, {}, {}, {}, {}, {}, {}, {}
+    used = list(cores) + [c for pr in comp.values() for c in pr]
     for (i, a), (ca, cb) in comp.items():
         head[ca] = head[cb] = na * i + a
         sib[ca], sib[cb] = cb, ca
         src[ca], src[cb] = [None] * NQ, [None] * NQ
+        for hc in (ca, cb):
+            idle = [c for c in range(SIM) if topo.chip(c) == topo.chip(hc) and topo.die(c) == topo.die(hc) and c not in used]
+            co[hc] = idle[0]
+            host[idle[0]] = hc
+            used.append(idle[0])
     for c in cores:
         dest[c] = []
         for t in range(NR):
             d = comp[(idx[c] ^ PERM[t // na], t % na)][0 if c in free else 1]
             dest[c].append(d)
             src[d][t // na] = c
-    return dest, src, head, sib
+        idle = [x for x in range(SIM) if topo.chip(x) == topo.chip(c) and x not in used]
+        far = [x for x in idle if topo.die(x) != topo.die(c)]
+        rel[c] = (far or idle)[0]
+        relof[rel[c]] = c
+        used.append(rel[c])
+    return {"dest": dest, "src": src, "head": head, "sib": sib, "co": co, "host": host, "rel": rel, "relof": relof}
 
 
 def _send_engines(topo, core, order, p):
@@ -101,123 +118,201 @@ def _send_engines(topo, core, order, p):
     return [use[0:n], use[n:2 * n]]
 
 
-def _rank_side(g, core, T, topo, dest, src, head, sib):
+def _relay_engines(topo, pl, r):
+    off = _engines(topo, r, pl["dest"][r])
+    return [e for e in _engines(topo, r, [pl["rel"][r]]) if e not in off]
+
+
+def _d_engines(topo, pl, d):
+    return _engines(topo, d, [pl["co"][pl["sib"][d]], pl["co"][d]])
+
+
+def _f_engines(topo, pl, d):
+    return _engines(topo, pl["co"][d], pl["src"][d] + [d])
+
+
+def _f_chip_engines(topo, pl, d):
+    off = _f_engines(topo, pl, d)
+    return [e for e in _engines(topo, pl["co"][d], [d]) if e not in off]
+
+
+def _res_engines(topo, pl, d, p):
+    fc, src = pl["co"][d], pl["src"][d]
+    off = _f_engines(topo, pl, d)
+    slots = list(range(OB * (p // OB), OB * (p // OB) + OB))
+    chip = [[e for e in _engines(topo, fc, [src[s]]) if e not in off] for s in slots]
+    mine = chip[slots.index(p)]
+    if mine:
+        return mine
+    outs = [s for i, s in enumerate(slots) if not chip[i]]
+    n = len(off) // len(outs)
+    i = outs.index(p)
+    return off[n * i:n * (i + 1)]
+
+
+def _rank_side(g, core, T, topo, pl):
     sem = T.sem
-    order = dest[core]
+    order = pl["dest"][core]
+    head, co = pl["head"], pl["co"]
     heads = [head[d] for d in order]
     half = NR // 2
     halves = [heads[0] // half, 1 - heads[0] // half]
     raw = (T.qr, T.kr, T.vr)
     inp = (T.q, T.k, T.v)
     qs = (g.sync, g.scalar)
-    n = 0
-    for pc, ts in enumerate(PIECES):
+    for n, (pc, x) in enumerate(LOADS):
+        ts = PIECES[pc]
         c0 = B * min(heads[t] for t in ts)
         c1 = c0 + B * len(ts)
-        for x in range(3):
-            qs[n % 2].dma_start(raw[x][:, c0:c1], inp[x][:, c0:c1]).then_inc(sem["ld%d%d" % (pc, x)], 16)
-            n += 1
-    packed = [0] * NR
+        qs[n % 2].dma_start(raw[x][:, c0:c1], inp[x][:, c0:c1]).then_inc(sem["ld%d%d" % (pc, x)], 16)
     for pc, ts in enumerate(PIECES):
         for t0 in range(ts[0], ts[-1] + 1, 2):
-            for x in range(3):
-                if x == 0 and t0 // 2 == QFIRST:
-                    continue
-                if t0 == ts[0]:
+            for x in ((0, 1, 2) if t0 // 2 == BUNDLE else (1, 2)):
+                if t0 == ts[0] or x == 0:
                     g.vector.wait_ge(sem["ld%d%d" % (pc, x)], 16)
                 for t in (t0, t0 + 1):
                     h = heads[t]
-                    g.vector.tensor_copy(T.pack[:, W * t + B * x:W * t + B * x + B],
-                                         raw[x][:, B * h:B * h + B]).then_inc(sem["pk%d" % t], 1)
-                    packed[t] += 1
+                    if t0 // 2 == BUNDLE:
+                        o = T.bsrc[:, 3 * B * (t - t0) + B * x:3 * B * (t - t0) + B * (x + 1)]
+                    else:
+                        o = T.pack[:, W * t + B * (x - 1):W * t + B * x]
+                    g.vector.tensor_copy(o, raw[x][:, B * h:B * h + B]).then_inc(sem["pk%d" % t], 1)
 
     total = [0]
 
-    def send(p, c0, c1, rs, unpacked):
+    def send_q(p):
         es = _send_engines(topo, core, order, p)
         trs = []
         for i in range(2):
             t = 2 * p + i
-            rid, pid, _se = topo.addr(order[t])
-            s = T.qr[:, B * heads[t]:B * heads[t] + B] if unpacked else T.pack[:, W * t + c0:W * t + c1]
-            trs.append(RemoteDMATransfer(dst_ids=[DstId(rid=rid, pnc=pid)], dma_engine_mask=_mask(es[i]), remote_sem=rs,
-                                         src=s, dst=T.land[:, W * p + c0:W * p + c1]))
+            rid, pid, _se = topo.addr(co[order[t]])
+            trs.append(RemoteDMATransfer(dst_ids=[DstId(rid=rid, pnc=pid)], dma_engine_mask=_mask(es[i]),
+                                         remote_sem=sem["qi%d" % p], src=T.qr[:, B * heads[t]:B * heads[t] + B],
+                                         dst=T.qa[:, B * p:B * p + B]))
             total[0] += len(es[i])
         g.remote_dma_fused(trs, local_sem=sem.sent)
 
-    for p in range(NQ):
-        if p == QFIRST:
-            g.wait_ge(sem["ld%d%d" % (0, 0)], 16)
-            send(p, 0, B, sem["in%d" % p], True)
-        for t in (2 * p, 2 * p + 1):
-            g.wait_ge(sem["pk%d" % t], packed[t])
-        if p == QFIRST:
-            send(p, B, W, sem["kn%d" % p], False)
-        elif p == KFIRST:
-            send(p, B, W, sem["kn%d" % p], False)
-            send(p, 0, B, sem["in%d" % p], False)
-        else:
-            send(p, 0, W, sem["in%d" % p], False)
+    def relay_q(p):
+        es = _relay_engines(topo, pl, core)
+        c0 = B * min(heads[2 * p], heads[2 * p + 1])
+        rid, pid, _se = topo.addr(pl["rel"][core])
+        g.remote_dma(out_ap=T.rq[:], in_ap=T.qr[:, c0:c0 + 2 * B], remote_sem=sem.rqs, local_sem=sem.sent,
+                     pid=pid, routing_id=rid, dma_engine_mask=_mask(es))
+        total[0] += len(es)
+
+    def send_kv(p):
+        es = _send_engines(topo, core, order, p)
+        trs = []
+        for i in range(2):
+            t = 2 * p + i
+            g.wait_ge(sem["pk%d" % t], 3 if p == BUNDLE else 2)
+            rid, pid, _se = topo.addr(order[t])
+            trs.append(RemoteDMATransfer(dst_ids=[DstId(rid=rid, pnc=pid)], dma_engine_mask=_mask(es[i]),
+                                         remote_sem=sem["kn%d" % p],
+                                         src=T.bsrc[:, 3 * B * i:3 * B * (i + 1)] if p == BUNDLE else T.pack[:, W * t:W * (t + 1)],
+                                         dst=T.bun[:] if p == BUNDLE else T.kv[:, W * p:W * (p + 1)]))
+            total[0] += len(es[i])
+        g.remote_dma_fused(trs, local_sem=sem.sent)
+
+    g.wait_ge(sem.ld00, 16)
+    send_q(0)
+    g.wait_ge(sem.ld20, 16)
+    relay_q(RELAY)
+    send_kv(0)
+    g.wait_ge(sem.ld10, 16)
+    send_q(1)
+    send_kv(1)
+    send_kv(2)
+    send_kv(3)
     g.wait_ge(sem.sent, total[0])
     for n, a in enumerate(halves):
         want = 0
         for d in order:
             if head[d] // half == a:
-                want += len(_engines(topo, d, src[d] + [sib[d]])) // OB
+                want += len(_res_engines(topo, pl, d, order.index(d) // 2))
         q = qs[n]
         q.wait_ge(sem["ya%d" % a], want)
         q.dma_start(T.y[:, half * B * a:half * B * (a + 1)], T.yb[:, half * B * a:half * B * (a + 1)]).then_inc(sem["st%d" % a], 16)
         q.wait_ge(sem["st%d" % a], 16)
 
 
-def _helper_side(g, core, T, topo, dest, src, head, sib):
+def _relay_side(g, core, T, topo, pl):
+    sem = T.sem
+    r = pl["relof"][core]
+    order = pl["dest"][r]
+    p = RELAY
+    hs = [pl["head"][order[2 * p + i]] for i in range(2)]
+    es = _send_engines(topo, core, order, p)
+    trs = []
+    for i in range(2):
+        rid, pid, _se = topo.addr(pl["co"][order[2 * p + i]])
+        c = B * (hs[i] - min(hs))
+        trs.append(RemoteDMATransfer(dst_ids=[DstId(rid=rid, pnc=pid)], dma_engine_mask=_mask(es[i]), remote_sem=sem["qi%d" % p],
+                                     src=T.rq[:, c:c + B], dst=T.qa[:, B * p:B * p + B]))
+    g.wait_ge(sem.rqs, len(_relay_engines(topo, pl, r)))
+    g.remote_dma_fused(trs, local_sem=sem.sent)
+    g.wait_ge(sem.sent, len(es[0]) + len(es[1]))
+
+
+def _helper_side(g, core, T, topo, pl, is_d):
     sem = T.sem
     te, ve = g.tensor, g.vector
-    h = head[core]
+    dc = core if is_d else pl["host"][core]
+    fc = pl["co"][dc]
+    h = pl["head"][dc]
+    src, dest, sib = pl["src"][dc], pl["dest"], pl["sib"][dc]
     obank = (T.o0, T.o1)
     sp = [T["sp%d" % b] for b in range(NSP)]
-    eng = _engines(topo, core, src[core] + [sib[core]])
-    seng = _engines(topo, sib[core], src[sib[core]] + [core])
+    deng = _d_engines(topo, pl, dc)
+    feng = _f_engines(topo, pl, dc)
+    fchip = _f_chip_engines(topo, pl, dc)
 
-    def arrived(p):
-        r = src[core][p]
-        return len(_send_engines(topo, r, dest[r], p)[dest[r].index(core) % 2])
+    def from_rank(p, relayed):
+        r = src[p]
+        return len(_send_engines(topo, pl["rel"][r] if relayed else r, dest[r], p)[dest[r].index(dc) % 2])
+
+    def arrival(ev):
+        kind, p = ev
+        if is_d:
+            if kind == "Q" and p != BUNDLE:
+                return (sem.qf0, len(feng)) if p < 2 else (sem.qf1, len(fchip))
+            return sem["kn%d" % p], from_rank(p, False)
+        if kind == "Q":
+            return sem["qi%d" % p], (len(deng) if p == BUNDLE else from_rank(p, p == RELAY))
+        return sem["kn%d" % p], len(_d_engines(topo, pl, sib))
 
     def q_(r):
-        return T.land[:, W * r:W * r + B]
+        return T.bun[:, 0:B] if is_d and r == BUNDLE else T.qa[:, B * r:B * r + B]
 
-    def k_(kv):
-        c = W * kv[1] + B if kv[0] == "D" else 2 * B * kv[1]
-        return (T.land if kv[0] == "D" else T.fw)[:, c:c + B]
+    def k_(p):
+        return T.bun[:, B:2 * B] if is_d and p == BUNDLE else T.kv[:, W * p:W * p + B]
 
-    def v_(kv):
-        c = W * kv[1] + 2 * B if kv[0] == "D" else 2 * B * kv[1] + B
-        return (T.land if kv[0] == "D" else T.fw)[:, c:c + B]
+    def v_(p):
+        return T.bun[:, 2 * B:3 * B] if is_d and p == BUNDLE else T.kv[:, W * p + B:W * p + W]
 
-    tiles, have_q, have_kv = [], [], []
-    for ei, ev in enumerate(EVENTS):
-        blocks = []
-        if ev[0] != "Q":
-            kv = ("F" if ev[0] == "F" else "D", ev[1])
-            blocks += [(kv, r) for r in have_q]
-            have_kv.append(kv)
-        if ev[0] in "DQ":
-            blocks += [(kv, ev[1]) for kv in have_kv]
+    tiles, have_q, have_kv, pend = [], [], [], []
+    for ev in (EVENTS_D if is_d else EVENTS_F):
+        pend.append(ev)
+        if ev[0] == "K":
+            blocks = [(ev[1], r) for r in sorted(have_q)]
+            have_kv.append(ev[1])
+        else:
+            blocks = [(p, ev[1]) for p in have_kv]
             have_q.append(ev[1])
-        size = OB if ei == len(EVENTS) - 1 else TILE
-        for c in range(0, len(blocks), size):
-            tiles.append((ev, c == 0, blocks[c:c + size]))
+        for c in range(0, len(blocks), OB):
+            tiles.append((pend, blocks[c:c + OB]))
+            pend = []
     nt = len(tiles)
-    flush = [n for n in range(nt) if tiles[n][1] and tiles[n][0] not in NODRAIN]
+    flush = [n for n in range(nt) if any(ev not in (NODRAIN_D if is_d else NODRAIN_F) for ev in tiles[n][0])]
     oops, off, base = [], [], 0
-    for (ev, first, blocks) in tiles:
+    for (evs, blocks) in tiles:
         ops = []
-        for i, (kv, r) in enumerate(blocks):
+        for i, (p, r) in enumerate(blocks):
             last = ops[-1] if ops else None
-            if last and last[0] == kv and last[1] == r // OB and last[2] + last[3] == r % OB:
+            if last and last[0] == p and last[1] == r // OB and last[2] + last[3] == r % OB:
                 last[3] += 1
             else:
-                ops.append([kv, r // OB, r % OB, 1, base + i])
+                ops.append([p, r // OB, r % OB, 1, base + i])
         oops.append(ops)
         off.append(base)
         base += len(blocks)
@@ -233,28 +328,24 @@ def _helper_side(g, core, T, topo, dest, src, head, sib):
     scount = [0] * NSP
     swant, rwant = [], []
     for n in range(nt):
-        scount[n % NSP] += len(tiles[n][2])
+        scount[n % NSP] += len(tiles[n][1])
         swant.append(scount[n % NSP])
         rwant.append(n // NSP + 1)
 
     def emit_s(n):
-        ev, first, blocks = tiles[n]
-        if first:
-            if ev[0] == "F":
-                te.wait_ge(sem["fw%d" % ev[1]], len(seng))
-            if ev[0] in "DQ":
-                te.wait_ge(sem["in%d" % ev[1]], arrived(ev[1]))
-            if ev[0] == "K" or (ev[0] == "D" and ev[1] == QFIRST):
-                te.wait_ge(sem["kn%d" % ev[1]], arrived(ev[1]))
+        evs, blocks = tiles[n]
+        for ev in evs:
+            s, cnt = arrival(ev)
+            te.wait_ge(s, cnt)
         b = n % NSP
-        for i, (kv, r) in enumerate(blocks):
-            te.matmul(sp[b][:, B * i:B * i + B], k_(kv), q_(r), True, True).then_inc(sem["ss%d" % b], 1)
+        for i, (p, r) in enumerate(blocks):
+            te.matmul(sp[b][:, B * i:B * i + B], k_(p), q_(r), True, True).then_inc(sem["ss%d" % b], 1)
 
     def emit_o(n):
         te.wait_ge(sem["rl%d" % (n % NSP)], rwant[n])
-        for (kv, x, c, w, s) in oops[n]:
+        for (p, x, c, w, s) in oops[n]:
             seen[x] += 1
-            te.matmul(obank[x][:, B * c:B * (c + w)], v_(kv), T.sr[:, B * s:B * (s + w)], False,
+            te.matmul(obank[x][:, B * c:B * (c + w)], v_(p), T.sr[:, B * s:B * (s + w)], False,
                       seen[x] == ocount[x]).then_inc(sem["od%d" % x], 1)
 
     nxt = 0
@@ -273,35 +364,67 @@ def _helper_side(g, core, T, topo, dest, src, head, sib):
 
     for n in range(nt):
         b = n % NSP
-        w = B * len(tiles[n][2])
+        w = B * len(tiles[n][1])
         ve.wait_ge(sem["ss%d" % b], swant[n])
         ve.tensor_tensor(T.sr[:, B * off[n]:B * off[n] + w], sp[b][:, 0:w], T.zf[:, 0:w], AluOpType.max).then_inc(sem["rl%d" % b], 1)
     for x in range(2):
+        c0, c1 = OB * B * x, OB * B * (x + 1)
         ve.wait_ge(sem["od%d" % x], ocount[x])
-        ve.tensor_copy(T.ys[:, OB * B * x:OB * B * (x + 1)], obank[x][:, 0:OB * B]).then_inc(sem["cp%d" % x], 1)
+        if is_d:
+            ve.tensor_copy(T.ys[:, c0:c1], obank[x][:, 0:OB * B]).then_inc(sem["cp%d" % x], 1)
+        else:
+            ve.wait_ge(sem["pa%d" % x], len(deng))
+            ve.tensor_tensor(T.ys[:, c0:c1], obank[x][:, 0:OB * B], T.part[:, c0:c1], AluOpType.add).then_inc(sem["cp%d" % x], 1)
 
-    rid, pid, _se = topo.addr(sib[core])
-    for p in range(NQ):
-        g.wait_ge(sem["kn%d" % p] if p in (QFIRST, KFIRST) else sem["in%d" % p], arrived(p))
-        g.remote_dma(out_ap=T.fw[:, 2 * B * p:2 * B * (p + 1)], in_ap=T.land[:, W * p + B:W * p + W], remote_sem=sem["fw%d" % p],
-                     local_sem=sem.sent, pid=pid, routing_id=rid, dma_engine_mask=_mask(eng))
-    per = len(eng) // OB
-    for x in range(2):
-        trs = []
-        for i in range(OB):
-            p = OB * x + i
-            rid, pid, _se = topo.addr(src[core][p])
-            trs.append(RemoteDMATransfer(dst_ids=[DstId(rid=rid, pnc=pid)], dma_engine_mask=_mask(eng[per * i:per * (i + 1)]),
-                                         remote_sem=sem["ya%d" % (h // (NR // 2))], src=T.ys[:, B * p:B * p + B],
-                                         dst=T.yb[:, B * h:B * h + B]))
-        g.wait_ge(sem["cp%d" % x], 1)
-        g.remote_dma_fused(trs, local_sem=sem.sent)
-    g.wait_ge(sem.sent, NQ * len(eng) + NQ * per)
+    if is_d:
+        rid, pid, _se = topo.addr(pl["co"][sib])
+        rid2, pid2, _se = topo.addr(fc)
+        for p in range(NQ):
+            s, cnt = arrival(("K", p))
+            g.wait_ge(s, cnt)
+            g.remote_dma(out_ap=T.kv[:, W * p:W * (p + 1)], in_ap=T.bun[:, B:3 * B] if p == BUNDLE else T.kv[:, W * p:W * (p + 1)],
+                         remote_sem=sem["kn%d" % p], local_sem=sem.sent, pid=pid, routing_id=rid, dma_engine_mask=_mask(deng))
+            if p == BUNDLE:
+                g.remote_dma(out_ap=T.qa[:, B * p:B * (p + 1)], in_ap=T.bun[:, 0:B], remote_sem=sem["qi%d" % p],
+                             local_sem=sem.sent, pid=pid2, routing_id=rid2, dma_engine_mask=_mask(deng))
+        for x in range(2):
+            c0, c1 = OB * B * x, OB * B * (x + 1)
+            g.wait_ge(sem["cp%d" % x], 1)
+            g.remote_dma(out_ap=T.part[:, c0:c1], in_ap=T.ys[:, c0:c1], remote_sem=sem["pa%d" % x],
+                         local_sem=sem.sent, pid=pid2, routing_id=rid2, dma_engine_mask=_mask(deng))
+        g.wait_ge(sem.sent, (NQ + 3) * len(deng))
+    else:
+        rid, pid, _se = topo.addr(dc)
+        done = 0
+        for j, (ps, es) in enumerate((([0, 1], feng), ([3], fchip))):
+            for p in ps:
+                s, cnt = arrival(("Q", p))
+                g.wait_ge(s, cnt)
+            g.remote_dma(out_ap=T.qa[:, B * ps[0]:B * (ps[-1] + 1)], in_ap=T.qa[:, B * ps[0]:B * (ps[-1] + 1)],
+                         remote_sem=sem["qf%d" % j], local_sem=sem.sent, pid=pid, routing_id=rid, dma_engine_mask=_mask(es))
+            done += len(es)
+        for x in range(2):
+            trs = []
+            for i in range(OB):
+                p = OB * x + i
+                es = _res_engines(topo, pl, dc, p)
+                rid, pid, _se = topo.addr(src[p])
+                trs.append(RemoteDMATransfer(dst_ids=[DstId(rid=rid, pnc=pid)], dma_engine_mask=_mask(es),
+                                             remote_sem=sem["ya%d" % (h // (NR // 2))], src=T.ys[:, B * p:B * p + B],
+                                             dst=T.yb[:, B * h:B * h + B]))
+                done += len(es)
+            g.wait_ge(sem["cp%d" % x], 1)
+            g.remote_dma_fused(trs, local_sem=sem.sent)
+        g.wait_ge(sem.sent, done)
 
 
 def rank_program(g, core, T, topo):
-    dest, src, head, sib = _plan(T.cores, topo)
+    pl = _plan(T.cores, topo)
     if T.rank_of(core) is not None:
-        _rank_side(g, core, T, topo, dest, src, head, sib)
-    elif core in head:
-        _helper_side(g, core, T, topo, dest, src, head, sib)
+        _rank_side(g, core, T, topo, pl)
+    elif core in pl["head"]:
+        _helper_side(g, core, T, topo, pl, True)
+    elif core in pl["host"]:
+        _helper_side(g, core, T, topo, pl, False)
+    elif core in pl["relof"]:
+        _relay_side(g, core, T, topo, pl)

from concourse.bass import DstId, RemoteDMATransfer
from concourse.mybir import AluOpType

SIM = 64
NR = 8
NQ = NR // 2
B = 128
W = 2 * B
NSP = 6
OB = 2

SCRATCH = {
    "qr": ("sbuf", [128, NR * B], "bfloat16"),
    "kr": ("sbuf", [128, NR * B], "bfloat16"),
    "vr": ("sbuf", [128, NR * B], "bfloat16"),
    "pack": ("sbuf", [128, NR * W], "bfloat16"),
    "bsrc": ("sbuf", [128, 2 * 3 * B], "bfloat16"),
    "bun": ("sbuf", [128, 3 * B], "bfloat16"),
    "rq": ("sbuf", [128, 2 * B], "bfloat16"),
    "qa": ("sbuf", [128, NQ * B], "bfloat16"),
    "kv": ("sbuf", [128, NQ * W], "bfloat16"),
    "sr": ("sbuf", [128, NQ * NQ * B], "bfloat16"),
    "zb": ("sbuf", [128, OB * B], "bfloat16"),
    "zf": ("sbuf", [128, OB * B], "float32"),
    "ys": ("sbuf", [128, NQ * B], "bfloat16"),
    "part": ("sbuf", [128, NQ * B], "bfloat16"),
    "yb": ("sbuf", [128, NR * B], "bfloat16"),
    "o0": ("psum", [128, 4 * B], "float32"),
    "o1": ("psum", [128, 4 * B], "float32"),
}
for _b in range(NSP):
    SCRATCH["sp%d" % _b] = ("psum", [128, 4 * B], "float32")

PIECES = [[0, 1], [2, 3], [4, 5, 6, 7]]
LOADS = [(0, 0), (2, 0), (0, 1), (0, 2), (1, 0), (1, 1), (1, 2), (2, 1), (2, 2)]

SEMAPHORES = (["ld%d%d" % (pc, x) for pc in range(len(PIECES)) for x in range(3)]
              + ["pk%d" % t for t in range(NR)] + ["qi%d" % p for p in range(NQ)] + ["qf%d" % j for j in range(NQ // 2)]
              + ["kn%d" % p for p in range(NQ)] + ["pa%d" % x for x in range(2)]
              + ["ss%d" % b for b in range(NSP)] + ["rl%d" % b for b in range(NSP)]
              + ["sent", "rqs", "ya0", "ya1", "st0", "st1", "zb", "zf", "od0", "od1", "cp0", "cp1"])

EVENTS_D = [("Q", 0), ("Q", 1), ("K", 0), ("K", 1), ("K", 2), ("Q", 2), ("Q", 3), ("K", 3)]
EVENTS_F = [("Q", 0), ("Q", 1), ("K", 0), ("K", 1), ("Q", 3), ("Q", 2), ("K", 2), ("K", 3)]
NODRAIN_D = [("K", 1), ("Q", 2), ("Q", 3)]
NODRAIN_F = [("K", 1), ("Q", 3), ("K", 2)]
BUNDLE = 2
RELAY = 3
PERM = [1, 0, 2, 3]


def _bits(m):
    return [e for e in range(m.bit_length()) if (m >> e) & 1]


def _mask(es):
    m = 0
    for e in es:
        m |= 1 << e
    return m


def _engines(topo, core, dsts):
    m = topo.mask(core, dsts[0])
    for d in dsts[1:]:
        m &= topo.mask(core, d)
    return _bits(m)


def _plan(cores, topo):
    cores = list(cores)
    bound = [c for c in cores if not all(topo.may_write(c, d) for d in cores if d != c)]
    free = [c for c in cores if c not in bound]
    nc = len(bound)
    mate = [[c for c in free if topo.mates(topo.chip(c), topo.chip(b))][0] for b in bound]
    idx = {}
    for i in range(nc):
        idx[bound[i]] = idx[mate[i]] = i
    comp = {}
    for i in range(nc):
        port = [[c for c in range(SIM) if topo.chip(c) == topo.chip(r) and c not in cores
                 and all(topo.may_write(c, d) for d in cores)] for r in (mate[i], bound[i])]
        dies = sorted(set(topo.die(c) for c in port[0]) & set(topo.die(c) for c in port[1]))
        for a, dd in enumerate(dies):
            comp[(i, a)] = tuple([c for c in pl if topo.die(c) == dd][0] for pl in port)
    na = len(comp) // nc
    dest, src, head, sib, co, host, rel, relof = {}, {}, {}, {}, {}, {}, {}, {}
    used = list(cores) + [c for pr in comp.values() for c in pr]
    for (i, a), (ca, cb) in comp.items():
        head[ca] = head[cb] = na * i + a
        sib[ca], sib[cb] = cb, ca
        src[ca], src[cb] = [None] * NQ, [None] * NQ
        for hc in (ca, cb):
            idle = [c for c in range(SIM) if topo.chip(c) == topo.chip(hc) and topo.die(c) == topo.die(hc) and c not in used]
            co[hc] = idle[0]
            host[idle[0]] = hc
            used.append(idle[0])
    for c in cores:
        dest[c] = []
        for t in range(NR):
            d = comp[(idx[c] ^ PERM[t // na], t % na)][0 if c in free else 1]
            dest[c].append(d)
            src[d][t // na] = c
        idle = [x for x in range(SIM) if topo.chip(x) == topo.chip(c) and x not in used]
        far = [x for x in idle if topo.die(x) != topo.die(c)]
        rel[c] = (far or idle)[0]
        relof[rel[c]] = c
        used.append(rel[c])
    return {"dest": dest, "src": src, "head": head, "sib": sib, "co": co, "host": host, "rel": rel, "relof": relof}


def _send_engines(topo, core, order, p):
    off = _engines(topo, core, order)
    pair = order[2 * p:2 * p + 2]
    rest = [e for e in _engines(topo, core, pair) if e not in off]
    use = rest if len(rest) >= len(off) else off
    n = len(off) // 2
    return [use[0:n], use[n:2 * n]]


def _relay_engines(topo, pl, r):
    off = _engines(topo, r, pl["dest"][r])
    return [e for e in _engines(topo, r, [pl["rel"][r]]) if e not in off]


def _d_engines(topo, pl, d):
    return _engines(topo, d, [pl["co"][pl["sib"][d]], pl["co"][d]])


def _f_engines(topo, pl, d):
    return _engines(topo, pl["co"][d], pl["src"][d] + [d])


def _f_chip_engines(topo, pl, d):
    off = _f_engines(topo, pl, d)
    return [e for e in _engines(topo, pl["co"][d], [d]) if e not in off]


def _res_engines(topo, pl, d, p):
    fc, src = pl["co"][d], pl["src"][d]
    off = _f_engines(topo, pl, d)
    slots = list(range(OB * (p // OB), OB * (p // OB) + OB))
    chip = [[e for e in _engines(topo, fc, [src[s]]) if e not in off] for s in slots]
    mine = chip[slots.index(p)]
    if mine:
        return mine
    outs = [s for i, s in enumerate(slots) if not chip[i]]
    n = len(off) // len(outs)
    i = outs.index(p)
    return off[n * i:n * (i + 1)]


def _rank_side(g, core, T, topo, pl):
    sem = T.sem
    order = pl["dest"][core]
    head, co = pl["head"], pl["co"]
    heads = [head[d] for d in order]
    half = NR // 2
    halves = [heads[0] // half, 1 - heads[0] // half]
    raw = (T.qr, T.kr, T.vr)
    inp = (T.q, T.k, T.v)
    qs = (g.sync, g.scalar)
    for n, (pc, x) in enumerate(LOADS):
        ts = PIECES[pc]
        c0 = B * min(heads[t] for t in ts)
        c1 = c0 + B * len(ts)
        qs[n % 2].dma_start(raw[x][:, c0:c1], inp[x][:, c0:c1]).then_inc(sem["ld%d%d" % (pc, x)], 16)
    for pc, ts in enumerate(PIECES):
        for t0 in range(ts[0], ts[-1] + 1, 2):
            for x in ((0, 1, 2) if t0 // 2 == BUNDLE else (1, 2)):
                if t0 == ts[0] or x == 0:
                    g.vector.wait_ge(sem["ld%d%d" % (pc, x)], 16)
                for t in (t0, t0 + 1):
                    h = heads[t]
                    if t0 // 2 == BUNDLE:
                        o = T.bsrc[:, 3 * B * (t - t0) + B * x:3 * B * (t - t0) + B * (x + 1)]
                    else:
                        o = T.pack[:, W * t + B * (x - 1):W * t + B * x]
                    g.vector.tensor_copy(o, raw[x][:, B * h:B * h + B]).then_inc(sem["pk%d" % t], 1)

    total = [0]

    def send_q(p):
        es = _send_engines(topo, core, order, p)
        trs = []
        for i in range(2):
            t = 2 * p + i
            rid, pid, _se = topo.addr(co[order[t]])
            trs.append(RemoteDMATransfer(dst_ids=[DstId(rid=rid, pnc=pid)], dma_engine_mask=_mask(es[i]),
                                         remote_sem=sem["qi%d" % p], src=T.qr[:, B * heads[t]:B * heads[t] + B],
                                         dst=T.qa[:, B * p:B * p + B]))
            total[0] += len(es[i])
        g.remote_dma_fused(trs, local_sem=sem.sent)

    def relay_q(p):
        es = _relay_engines(topo, pl, core)
        c0 = B * min(heads[2 * p], heads[2 * p + 1])
        rid, pid, _se = topo.addr(pl["rel"][core])
        g.remote_dma(out_ap=T.rq[:], in_ap=T.qr[:, c0:c0 + 2 * B], remote_sem=sem.rqs, local_sem=sem.sent,
                     pid=pid, routing_id=rid, dma_engine_mask=_mask(es))
        total[0] += len(es)

    def send_kv(p):
        es = _send_engines(topo, core, order, p)
        trs = []
        for i in range(2):
            t = 2 * p + i
            g.wait_ge(sem["pk%d" % t], 3 if p == BUNDLE else 2)
            rid, pid, _se = topo.addr(order[t])
            trs.append(RemoteDMATransfer(dst_ids=[DstId(rid=rid, pnc=pid)], dma_engine_mask=_mask(es[i]),
                                         remote_sem=sem["kn%d" % p],
                                         src=T.bsrc[:, 3 * B * i:3 * B * (i + 1)] if p == BUNDLE else T.pack[:, W * t:W * (t + 1)],
                                         dst=T.bun[:] if p == BUNDLE else T.kv[:, W * p:W * (p + 1)]))
            total[0] += len(es[i])
        g.remote_dma_fused(trs, local_sem=sem.sent)

    g.wait_ge(sem.ld00, 16)
    send_q(0)
    g.wait_ge(sem.ld20, 16)
    relay_q(RELAY)
    send_kv(0)
    g.wait_ge(sem.ld10, 16)
    send_q(1)
    send_kv(1)
    send_kv(2)
    send_kv(3)
    g.wait_ge(sem.sent, total[0])
    for n, a in enumerate(halves):
        want = 0
        for d in order:
            if head[d] // half == a:
                want += len(_res_engines(topo, pl, d, order.index(d) // 2))
        q = qs[n]
        q.wait_ge(sem["ya%d" % a], want)
        q.dma_start(T.y[:, half * B * a:half * B * (a + 1)], T.yb[:, half * B * a:half * B * (a + 1)]).then_inc(sem["st%d" % a], 16)
        q.wait_ge(sem["st%d" % a], 16)


def _relay_side(g, core, T, topo, pl):
    sem = T.sem
    r = pl["relof"][core]
    order = pl["dest"][r]
    p = RELAY
    hs = [pl["head"][order[2 * p + i]] for i in range(2)]
    es = _send_engines(topo, core, order, p)
    trs = []
    for i in range(2):
        rid, pid, _se = topo.addr(pl["co"][order[2 * p + i]])
        c = B * (hs[i] - min(hs))
        trs.append(RemoteDMATransfer(dst_ids=[DstId(rid=rid, pnc=pid)], dma_engine_mask=_mask(es[i]), remote_sem=sem["qi%d" % p],
                                     src=T.rq[:, c:c + B], dst=T.qa[:, B * p:B * p + B]))
    g.wait_ge(sem.rqs, len(_relay_engines(topo, pl, r)))
    g.remote_dma_fused(trs, local_sem=sem.sent)
    g.wait_ge(sem.sent, len(es[0]) + len(es[1]))


def _helper_side(g, core, T, topo, pl, is_d):
    sem = T.sem
    te, ve = g.tensor, g.vector
    dc = core if is_d else pl["host"][core]
    fc = pl["co"][dc]
    h = pl["head"][dc]
    src, dest, sib = pl["src"][dc], pl["dest"], pl["sib"][dc]
    obank = (T.o0, T.o1)
    sp = [T["sp%d" % b] for b in range(NSP)]
    deng = _d_engines(topo, pl, dc)
    feng = _f_engines(topo, pl, dc)
    fchip = _f_chip_engines(topo, pl, dc)

    def from_rank(p, relayed):
        r = src[p]
        return len(_send_engines(topo, pl["rel"][r] if relayed else r, dest[r], p)[dest[r].index(dc) % 2])

    def arrival(ev):
        kind, p = ev
        if is_d:
            if kind == "Q" and p != BUNDLE:
                return (sem.qf0, len(feng)) if p < 2 else (sem.qf1, len(fchip))
            return sem["kn%d" % p], from_rank(p, False)
        if kind == "Q":
            return sem["qi%d" % p], (len(deng) if p == BUNDLE else from_rank(p, p == RELAY))
        return sem["kn%d" % p], len(_d_engines(topo, pl, sib))

    def q_(r):
        return T.bun[:, 0:B] if is_d and r == BUNDLE else T.qa[:, B * r:B * r + B]

    def k_(p):
        return T.bun[:, B:2 * B] if is_d and p == BUNDLE else T.kv[:, W * p:W * p + B]

    def v_(p):
        return T.bun[:, 2 * B:3 * B] if is_d and p == BUNDLE else T.kv[:, W * p + B:W * p + W]

    tiles, have_q, have_kv, pend = [], [], [], []
    for ev in (EVENTS_D if is_d else EVENTS_F):
        pend.append(ev)
        if ev[0] == "K":
            blocks = [(ev[1], r) for r in sorted(have_q)]
            have_kv.append(ev[1])
        else:
            blocks = [(p, ev[1]) for p in have_kv]
            have_q.append(ev[1])
        for c in range(0, len(blocks), OB):
            tiles.append((pend, blocks[c:c + OB]))
            pend = []
    nt = len(tiles)
    flush = [n for n in range(nt) if any(ev not in (NODRAIN_D if is_d else NODRAIN_F) for ev in tiles[n][0])]
    oops, off, base = [], [], 0
    for (evs, blocks) in tiles:
        ops = []
        for i, (p, r) in enumerate(blocks):
            last = ops[-1] if ops else None
            if last and last[0] == p and last[1] == r // OB and last[2] + last[3] == r % OB:
                last[3] += 1
            else:
                ops.append([p, r // OB, r % OB, 1, base + i])
        oops.append(ops)
        off.append(base)
        base += len(blocks)
    ocount = [1 + sum(1 for ops in oops for o in ops if o[1] == x) for x in range(2)]

    ve.memset(T.zb[:], 0.0).then_inc(sem.zb, 1)
    ve.memset(T.zf[:], 0.0).then_inc(sem.zf, 1)
    ve.wait_ge(sem.zf, 1)
    te.wait_ge(sem.zb, 1)
    for x in range(2):
        te.matmul(obank[x][:, 0:OB * B], T.zb[:, 0:B], T.zb[:], True, False).then_inc(sem["od%d" % x], 1)
    seen = [1, 1]
    scount = [0] * NSP
    swant, rwant = [], []
    for n in range(nt):
        scount[n % NSP] += len(tiles[n][1])
        swant.append(scount[n % NSP])
        rwant.append(n // NSP + 1)

    def emit_s(n):
        evs, blocks = tiles[n]
        for ev in evs:
            s, cnt = arrival(ev)
            te.wait_ge(s, cnt)
        b = n % NSP
        for i, (p, r) in enumerate(blocks):
            te.matmul(sp[b][:, B * i:B * i + B], k_(p), q_(r), True, True).then_inc(sem["ss%d" % b], 1)

    def emit_o(n):
        te.wait_ge(sem["rl%d" % (n % NSP)], rwant[n])
        for (p, x, c, w, s) in oops[n]:
            seen[x] += 1
            te.matmul(obank[x][:, B * c:B * (c + w)], v_(p), T.sr[:, B * s:B * (s + w)], False,
                      seen[x] == ocount[x]).then_inc(sem["od%d" % x], 1)

    nxt = 0
    for n in range(nt):
        if n in flush:
            while nxt < n:
                emit_o(nxt)
                nxt += 1
        emit_s(n)
        while nxt <= n - 2:
            emit_o(nxt)
            nxt += 1
    while nxt < nt:
        emit_o(nxt)
        nxt += 1

    for n in range(nt):
        b = n % NSP
        w = B * len(tiles[n][1])
        ve.wait_ge(sem["ss%d" % b], swant[n])
        ve.tensor_tensor(T.sr[:, B * off[n]:B * off[n] + w], sp[b][:, 0:w], T.zf[:, 0:w], AluOpType.max).then_inc(sem["rl%d" % b], 1)
    for x in range(2):
        c0, c1 = OB * B * x, OB * B * (x + 1)
        ve.wait_ge(sem["od%d" % x], ocount[x])
        if is_d:
            ve.tensor_copy(T.ys[:, c0:c1], obank[x][:, 0:OB * B]).then_inc(sem["cp%d" % x], 1)
        else:
            ve.wait_ge(sem["pa%d" % x], len(deng))
            ve.tensor_tensor(T.ys[:, c0:c1], obank[x][:, 0:OB * B], T.part[:, c0:c1], AluOpType.add).then_inc(sem["cp%d" % x], 1)

    if is_d:
        rid, pid, _se = topo.addr(pl["co"][sib])
        rid2, pid2, _se = topo.addr(fc)
        for p in range(NQ):
            s, cnt = arrival(("K", p))
            g.wait_ge(s, cnt)
            g.remote_dma(out_ap=T.kv[:, W * p:W * (p + 1)], in_ap=T.bun[:, B:3 * B] if p == BUNDLE else T.kv[:, W * p:W * (p + 1)],
                         remote_sem=sem["kn%d" % p], local_sem=sem.sent, pid=pid, routing_id=rid, dma_engine_mask=_mask(deng))
            if p == BUNDLE:
                g.remote_dma(out_ap=T.qa[:, B * p:B * (p + 1)], in_ap=T.bun[:, 0:B], remote_sem=sem["qi%d" % p],
                             local_sem=sem.sent, pid=pid2, routing_id=rid2, dma_engine_mask=_mask(deng))
        for x in range(2):
            c0, c1 = OB * B * x, OB * B * (x + 1)
            g.wait_ge(sem["cp%d" % x], 1)
            g.remote_dma(out_ap=T.part[:, c0:c1], in_ap=T.ys[:, c0:c1], remote_sem=sem["pa%d" % x],
                         local_sem=sem.sent, pid=pid2, routing_id=rid2, dma_engine_mask=_mask(deng))
        g.wait_ge(sem.sent, (NQ + 3) * len(deng))
    else:
        rid, pid, _se = topo.addr(dc)
        done = 0
        for j, (ps, es) in enumerate((([0, 1], feng), ([3], fchip))):
            for p in ps:
                s, cnt = arrival(("Q", p))
                g.wait_ge(s, cnt)
            g.remote_dma(out_ap=T.qa[:, B * ps[0]:B * (ps[-1] + 1)], in_ap=T.qa[:, B * ps[0]:B * (ps[-1] + 1)],
                         remote_sem=sem["qf%d" % j], local_sem=sem.sent, pid=pid, routing_id=rid, dma_engine_mask=_mask(es))
            done += len(es)
        for x in range(2):
            trs = []
            for i in range(OB):
                p = OB * x + i
                es = _res_engines(topo, pl, dc, p)
                rid, pid, _se = topo.addr(src[p])
                trs.append(RemoteDMATransfer(dst_ids=[DstId(rid=rid, pnc=pid)], dma_engine_mask=_mask(es),
                                             remote_sem=sem["ya%d" % (h // (NR // 2))], src=T.ys[:, B * p:B * p + B],
                                             dst=T.yb[:, B * h:B * h + B]))
                done += len(es)
            g.wait_ge(sem["cp%d" % x], 1)
            g.remote_dma_fused(trs, local_sem=sem.sent)
        g.wait_ge(sem.sent, done)


def rank_program(g, core, T, topo):
    pl = _plan(T.cores, topo)
    if T.rank_of(core) is not None:
        _rank_side(g, core, T, topo, pl)
    elif core in pl["head"]:
        _helper_side(g, core, T, topo, pl, True)
    elif core in pl["host"]:
        _helper_side(g, core, T, topo, pl, False)
    elif core in pl["relof"]:
        _relay_side(g, core, T, topo, pl)
